import numpy as np
import ml_dtypes


def mxq(x, axis, fmt="e4m3"):
    dtype, down = {"e4m3": (ml_dtypes.float8_e4m3fn, 7), "e5m2": (ml_dtypes.float8_e5m2, 14)}[fmt]
    v = np.moveaxis(np.asarray(x, np.float32).astype(ml_dtypes.bfloat16).astype(np.float64), axis, -1)
    blocks = v.reshape(v.shape[:-1] + (-1, 32))
    amax = np.abs(blocks).max(-1, keepdims=True)
    byte = np.maximum(np.where(amax > 0, np.frexp(amax)[1] - 1 + 127, 0) - down, 1)
    scale = np.exp2(byte - 127.0)
    codes = (blocks / scale).astype(np.float32).astype(dtype).astype(np.float64)
    return np.moveaxis((codes * scale).reshape(v.shape), -1, axis)


WIDE = False


def mx_kscale(k):
    if not WIDE:
        return np.ones(k)
    levels = np.array([10, -10, 5, -5, 0])
    if k % 512:
        return np.exp2(np.random.permutation(np.resize(levels, k // 32))).repeat(32)
    a = np.empty((k // 512, 16))
    for p in range(k // 512):
        a[p, :8] = np.random.permutation(np.resize(levels, 8))
        for g in range(8):
            far = levels[np.abs(levels - a[p, g]) >= 10]
            a[p, g + 8] = far[np.random.randint(len(far))]
    return np.exp2(a.ravel()).repeat(32)


BF16 = ml_dtypes.bfloat16


def bf(x):
    return np.asarray(x, np.float32).astype(BF16)


def f64(x):
    return np.asarray(x).astype(np.float64)


E2M1 = np.array([0.0, 0.5, 1.0, 1.5, 2.0, 3.0, 4.0, 6.0, -0.0, -0.5, -1.0, -1.5, -2.0, -3.0, -4.0, -6.0])


def pack_weight(w, fmt):
    k, n = w.shape
    w = f64(bf(w)).reshape(k // 32, 32, n)
    amax = np.abs(w).max(1)
    if fmt == "e4m3":
        byte = np.frexp(amax)[1] - 1 + 127 - 7
    else:
        mant, ex = np.frexp(amax / 6.0)
        byte = np.where(mant > 0.5, ex, ex - 1) + 127
    byte = np.clip(np.where(amax > 0, byte, 1), 1, 254)
    scaled = (w * np.exp2(127.0 - byte)[:, None, :]).reshape(k, n).astype(np.float32)
    by_word = np.ascontiguousarray(scaled.reshape(k // 512, 128, 4, n).transpose(0, 1, 3, 2))
    if fmt == "e4m3":
        words = by_word.astype(ml_dtypes.float8_e4m3fn).view(np.uint8)
    else:
        c = by_word.astype(ml_dtypes.float4_e2m1fn).view(np.uint8) & 0xF
        words = c[..., 0::2] | (c[..., 1::2] << 4)
    return np.ascontiguousarray(words), np.ascontiguousarray(byte.astype(np.uint8).reshape(k // 512, 16, n))


def unpack_weight(words, scales, fmt):
    g, p, n, _ = words.shape
    if fmt == "e4m3":
        vals = np.ascontiguousarray(words).view(ml_dtypes.float8_e4m3fn).astype(np.float64)
    else:
        nib = np.empty((g, p, n, 4), np.uint8)
        nib[..., 0::2] = words & 0xF
        nib[..., 1::2] = words >> 4
        vals = E2M1[nib]
    vals = vals * np.repeat(np.exp2(scales.astype(np.float64) - 127.0), 8, axis=1)[..., None]
    return vals.transpose(0, 1, 3, 2).reshape(g * 512, n)
def pack4(w):
    words, scales = pack_weight(w, "e2m1")
    return words.reshape(words.shape[0], 128, -1), scales


def unpack4(words, scales):
    return unpack_weight(words.reshape(words.shape[0], 128, -1, 2), scales, "e2m1")


def planes(Y):
    n, m = Y.shape
    b = f64(bf(Y)).reshape(n // 32, 32, m)
    amax = np.abs(b).max(1)
    byte = np.clip(np.where(amax > 0, np.frexp(amax)[1] - 1 + 127 - 7, 1), 1, 254)
    codes = (b * np.exp2(127.0 - byte)[:, None, :]).reshape(n, m).astype(np.float32).astype(ml_dtypes.float8_e4m3fn).view(np.uint8)
    words = codes.reshape(n // 512, 128, 4, m).transpose(0, 1, 3, 2)
    return np.ascontiguousarray(words), np.ascontiguousarray(byte.astype(np.uint8).reshape(n // 512, 16, m))


P, K, L, F = 2048, 1024, 1536, 512

DIFFUSE = 0.7


def setup_inputs():
    s = mx_kscale(K)
    t = mx_kscale(L)
    normals = np.random.randn(K, P) * s[:, None]
    halves = np.random.randn(K, L) / np.sqrt(K) / s[:, None] * t[None, :]
    nrm_words, nrm_scales = pack4(normals)
    half_words, half_scales = pack4(halves)
    spread = np.exp(0.8 * np.random.randn(F))
    radiance = np.random.randn(L, F) / np.sqrt(L) * spread[None, :] / np.square(t)[:, None]
    specular = np.exp(0.3 * np.random.randn(P))
    diffuse = DIFFUSE * np.random.randn(P, F) * spread[None, :]
    return {"nrm_words": nrm_words, "nrm_scales": nrm_scales,
            "half_words": half_words, "half_scales": half_scales,
            "radiance": bf(radiance), "specular": bf(specular), "diffuse": bf(diffuse)}


def reference(nrm_words, nrm_scales, half_words, half_scales, radiance, specular, diffuse):
    A = unpack4(nrm_words, nrm_scales)
    H = unpack4(half_words, half_scales)
    D = A.T @ H
    S = np.square(np.maximum(D, 0.0))
    C = mxq(S, 1, "e4m3") @ mxq(f64(radiance), 0, "e4m3")
    y = f64(specular)[:, None] * C + f64(diffuse)
    Y = y.T
    words, scales = planes(Y)
    return y, words, scales

@@ -1,0 +1,311 @@
+from contextlib import ExitStack
+
+import concourse.mybir as mybir
+from concourse.masks import make_identity
+
+POINTS, FEATS, LIGHTS, RAD = 2048, 1024, 1536, 512
+FLOPS = 2 * POINTS * FEATS * LIGHTS + 2 * POINTS * LIGHTS * RAD
+
+F32 = mybir.dt.float32
+BF16 = mybir.dt.bfloat16
+I32 = mybir.dt.int32
+U32 = mybir.dt.uint32
+U8 = mybir.dt.uint8
+FP8X4 = mybir.dt.float8_e4m3fn_x4
+FP4X4 = mybir.dt.float4_e2m1fn_x4
+ACT = mybir.ActivationFunctionType
+ALU = mybir.AluOpType
+
+P = 128
+CHUNK = 512
+CHUNKS = POINTS // CHUNK
+GROUPS = LIGHTS // 512
+KP = FEATS // 512
+TILES = CHUNK // P
+UNITS = CHUNKS * GROUPS
+BANKS = 8
+G_CAST = False
+G_RAD = False
+RB = 4
+WARM_S = True
+LAG = 3
+LA, LB, LQ, LG = 1, 1, 6, 1
+NS = 4
+NS0 = 6
+RAD0, RADSTEP = 5, 4
+SORT1 = 1
+TE, TS, TR, SP = 4, 1, 2, 2
+
+G_CAST = False
+G_RAD = False
+NS = 4
+NS0 = 6
+WARM_S = False
+
+
+def tile_blinn_phong_radiance_features_k5_kernel(
+    tc, nrm_words, nrm_scales, half_words, half_scales, radiance, specular, diffuse, out_0, out_1, out_2
+):
+    nc = tc.nc
+    with ExitStack() as ctx:
+        keep = ctx.enter_context(tc.tile_pool(name="keep", bufs=1))
+        work = ctx.enter_context(tc.tile_pool(name="work", bufs=3))
+        psum = ctx.enter_context(tc.psum_pool(name="psum", bufs=1))
+        ctx.enter_context(tc.manual_schedule())
+
+        taken = []
+
+        def next_bank():
+            bank = psum.tile([P, 512], F32, name="bank%d" % len(taken), tag="bank%d" % (len(taken) % BANKS))
+            taken.append(bank)
+            return bank
+
+        def kept(shape, dtype, name):
+            return keep.tile(shape, dtype, name=name, align_bytes=64)
+
+        hw_raw = [kept([P, KP, 1024], U8, "hw_raw%d" % g) for g in range(GROUPS)]
+        hs_raw = kept([P, KP, LIGHTS], U8, "hs_raw")
+        aw = [kept([P, KP, 2 * CHUNK], U8, "aw%d" % c) for c in range(CHUNKS)]
+        as_first = kept([P, KP, CHUNK], U8, "as_first")
+        as_rest = kept([P, KP, POINTS - CHUNK], U8, "as_rest")
+        rad_raw = [kept([P, 4, RAD], BF16, "rad_raw%d" % g) for g in range(GROUPS)]
+        dif = [kept([P, TILES, RAD], BF16, "dif%d" % c) for c in range(CHUNKS)]
+        spec_raw = kept([16, P], BF16, "spec_raw")
+        spec_rows = kept([P, P], F32, "spec_rows")
+        spec = kept([P, 16], F32, "spec")
+        ident = kept([P, P], F32, "ident")
+        warm = kept([P, 8], F32, "warm")
+        warm2 = kept([P, 8], F32, "warm2")
+
+        def load_words(queue, dst, words, block):
+            src = words.bitcast(I32)[:, :, 256 * block : 256 * (block + 1)]
+            queue.dma_start(out=dst[:].bitcast(I32), in_=src.rearrange("k p w -> p k w"))
+
+        def load_scales(queue, dst, scales, r, col0, cols):
+            src = scales.bitcast(I32).rearrange("k (q r) w -> r q k w", r=4)[r]
+            queue.dma_start(out=dst[:].bitcast(I32)[r:P:32], in_=src[:, :, col0 // 4 : (col0 + cols) // 4])
+
+        def load_radiance(g):
+            src = radiance[512 * g : 512 * (g + 1), :].rearrange("(j t b) f -> b j t f", t=4, b=4)
+            for b in range(4):
+                nc.sync.dma_start(out=rad_raw[g][b:P:4], in_=src[b])
+
+        def load_diffuse(c):
+            nc.sync.dma_start(out=dif[c][:], in_=diffuse[CHUNK * c : CHUNK * (c + 1), :].rearrange("(j p) f -> p j f", p=P))
+
+        nc.vector.memset(hs_raw[:].bitcast(I32), 0)
+        nc.vector.memset(as_first[:].bitcast(I32), 0)
+        if WARM_S:
+            nc.vector.memset(warm[:], 0.0)
+        nc.vector.memset(as_rest[:].bitcast(I32), 0)
+        if WARM_S:
+            nc.scalar.activation(out=warm2[:], in_=warm[:], func=ACT.Square)
+        load_words(nc.sync, hw_raw[0], half_words, 0)
+        load_words(nc.sync, aw[0], nrm_words, 0)
+        for r in range(4):
+            load_scales(nc.sync, hs_raw, half_scales, r, 0, LIGHTS)
+        for r in range(4):
+            load_scales(nc.sync, as_first, nrm_scales, r, 0, CHUNK)
+        load_words(nc.sync, hw_raw[1], half_words, 1)
+        load_words(nc.sync, hw_raw[2], half_words, 2)
+        load_radiance(0)
+        nc.sync.dma_start(out=spec_raw[:], in_=specular.rearrange("(n p) -> n p", p=P))
+        load_words(nc.sync, aw[1], nrm_words, 1)
+        for r in range(4):
+            load_scales(nc.sync, as_rest, nrm_scales, r, CHUNK, POINTS - CHUNK)
+        load_radiance(1)
+        load_radiance(2)
+        load_diffuse(0)
+        for c in range(2, CHUNKS):
+            load_words(nc.sync, aw[c], nrm_words, c)
+        for c in range(1, CHUNKS):
+            load_diffuse(c)
+
+        make_identity(nc, ident[:])
+        nc.gpsimd.memset(spec_rows[:], 0.0)
+        nc.gpsimd.tensor_copy(out=spec_rows[0:16, :], in_=spec_raw[:])
+
+        hw = [kept([P, KP, 4, 256], U8, "hw%d" % g) for g in range(GROUPS)]
+        hs = [kept([P, KP, 4, P], U8, "hs%d" % g) for g in range(GROUPS)]
+        rad_codes = [kept([P, RAD], U32, "rad_codes%d" % g) for g in range(GROUPS)]
+        rad_scales = [kept([P, RAD], U8, "rad_scales%d" % g) for g in range(GROUPS)]
+        rad_il = [kept([P, RAD, 4], BF16, "rad_il%d" % g) for g in range(GROUPS)]
+        s_codes = [kept([P, CHUNK], U32, "s_codes%d" % u) for u in range(UNITS)]
+        s_scales = [kept([P, CHUNK], U8, "s_scales%d" % u) for u in range(UNITS)]
+        y_codes = [kept([P, CHUNK], U32, "y_codes%d" % c) for c in range(CHUNKS)]
+        y_scales = kept([P, POINTS], U8, "y_scales")
+        relu_d, lobe, acc, y, y_pairs, turned, y_t = {}, {}, {}, {}, {}, {}, {}
+
+        def sort_lights(g):
+            nc.vector.tensor_copy(
+                out=hw[g][:].bitcast(I32).rearrange("p k t (j w) -> p k t j w", w=2),
+                in_=hw_raw[g][:].bitcast(I32).rearrange("p k (j t w) -> p k t j w", t=4, w=2),
+            )
+            nc.vector.tensor_copy(
+                out=hs[g][:].bitcast(I32),
+                in_=hs_raw[:].bitcast(I32)[:, :, P * g : P * (g + 1)].rearrange("p k (j t) -> p k t j", t=4),
+            )
+
+        def interleave_radiance(g, f0, f1):
+            dst = rad_il[g][:, f0:f1, :].rearrange("p (c i) t -> p c t i", i=4)
+            src = rad_raw[g][:, :, f0:f1].rearrange("p t (c i) -> p c t i", i=4)
+            if G_RAD:
+                nc.gpsimd.tensor_scalar(out=rad_il[g][:, f0:f1, :], in0=rad_raw[g][:, :, f0:f1].rearrange("p t f -> p f t"), scalar1=1.0, scalar2=0.0, op0=ALU.mult, op1=ALU.add)
+            else:
+                nc.vector.tensor_copy(out=dst, in_=src)
+
+        def quantize_radiance(g):
+            nc.vector.quantize_mx(out=rad_codes[g][:].bitcast(FP8X4), scales=rad_scales[g][:],
+                                  in_=rad_il[g][:].rearrange("p f t -> p (f t)"))
+
+        def spread_specular():
+            bank = next_bank()
+            nc.tensor.transpose(bank[:, 0:P], spec_rows[:], ident[:])
+            nc.scalar.copy(out=spec[:], in_=bank[:, 0:16])
+
+        def dots(u, t):
+            c, g = divmod(u, GROUPS)
+            bank = next_bank()
+            acc["d", u, t] = bank
+            for k in range(KP):
+                a_scale = as_first[:, k, :] if c == 0 else as_rest[:, k, CHUNK * (c - 1) : CHUNK * c]
+                nc.tensor.matmul_mx(out=bank[:], lhsT=hw[g][:, k, t, :].bitcast(FP4X4), lhsT_scale=hs[g][:, k, t, :],
+                                    rhs=aw[c][:, k, :].bitcast(FP4X4), rhs_scale=a_scale, start=(k == 0), stop=(k == KP - 1))
+
+        def relu(u, t, on_scalar):
+            if t == 0:
+                relu_d[u] = work.tile([P, 4, CHUNK], F32, name="relu%d" % u, tag="relu", bufs=RB)
+            if on_scalar:
+                nc.scalar.activation(out=relu_d[u][:, t, :], in_=acc["d", u, t][:], func=ACT.Relu)
+            else:
+                nc.vector.tensor_scalar(out=relu_d[u][:, t, :], in0=acc["d", u, t][:], scalar1=0.0, scalar2=None, op0=ALU.max)
+
+        def square(u, c0, c1):
+            if c0 == 0:
+                lobe[u] = work.tile([P, CHUNK, 4], BF16, name="lobe%d" % u, tag="lobe", align_bytes=64)
+            cols = slice(c0, c1)
+            nc.scalar.activation(out=lobe[u][:, cols, :].rearrange("p (c i) t -> p c t i", i=2),
+                                 in_=relu_d[u][:, :, cols].rearrange("p t (c i) -> p c t i", i=2), func=ACT.Square)
+
+        def quantize_lobe(u, c0, c1):
+            nc.vector.quantize_mx(out=s_codes[u][:, c0:c1].bitcast(FP8X4), scales=s_scales[u][:, c0:c1],
+                                  in_=lobe[u][:, c0:c1, :].rearrange("p i t -> p (i t)"))
+
+        def shade(n, g0, g1):
+            c, j = divmod(n, TILES)
+            if g0 == 0:
+                acc["c", n] = next_bank()
+            cols = slice(P * j, P * (j + 1))
+            for g in range(g0, g1):
+                u = GROUPS * c + g
+                nc.tensor.matmul_mx(out=acc["c", n][:], lhsT=s_codes[u][:, cols].bitcast(FP8X4), lhsT_scale=s_scales[u][:, cols],
+                                    rhs=rad_codes[g][:].bitcast(FP8X4), rhs_scale=rad_scales[g][:], start=(g == 0), stop=(g == GROUPS - 1))
+
+        def finish(n):
+            c, j = divmod(n, TILES)
+            y[n] = work.tile([P, RAD], F32, name="y%d" % n, tag="y", bufs=6)
+            nc.vector.scalar_tensor_tensor(out=y[n][:], in0=acc["c", n][:], scalar=spec[:, n : n + 1], in1=dif[c][:, j, :],
+                                           op0=ALU.mult, op1=ALU.add)
+            nc.sync.dma_start(out=out_0[P * n : P * (n + 1), :], in_=y[n][:])
+
+        def round_pairs(n, on_scalar):
+            y_pairs[n] = work.tile([P, 2, P, 2], BF16, name="y_pairs%d" % n, tag="y_pairs", bufs=8)
+            src = y[n][:].rearrange("p (m u e) -> p u m e", u=2, e=2)
+            if on_scalar:
+                nc.scalar.copy(out=y_pairs[n][:], in_=src)
+            elif G_CAST:
+                nc.gpsimd.tensor_scalar(out=y_pairs[n][:], in0=src, scalar1=1.0, scalar2=0.0, op0=ALU.mult, op1=ALU.add)
+            else:
+                nc.vector.tensor_copy(out=y_pairs[n][:], in_=src)
+
+        def turn(n0, n1):
+            bank = next_bank()
+            turned[n0] = bank
+            for n in range(n0, n1):
+                words = y_pairs[n][:].rearrange("p u m e -> p u (m e)").bitcast(F32)
+                for u in range(2):
+                    col = P * (2 * (n - n0) + u)
+                    nc.tensor.transpose(bank[:, col : col + P], words[:, u, :], ident[:])
+
+        def gather(n0, n1):
+            c, j = divmod(n0, TILES)
+            if j == 0:
+                y_t[c] = work.tile([P, CHUNK, 4], BF16, name="y_t%d" % c, tag="y_t", bufs=2, align_bytes=64)
+            s = n1 - n0
+            dst = y_t[c][:, P * j : P * (j + s), :].bitcast(F32).rearrange("p (s i) u -> p s i u", s=s)
+            nc.scalar.copy(out=dst, in_=turned[n0][:, 0 : 2 * P * s].rearrange("p (s u i) -> p s i u", s=s, u=2))
+
+        words_out = out_1[0].rearrange("p m t -> p (m t)").bitcast(I32)
+
+        def quantize_result(c, c0, c1):
+            nc.vector.quantize_mx(out=y_codes[c][:, c0:c1].bitcast(FP8X4), scales=y_scales[:, CHUNK * c + c0 : CHUNK * c + c1],
+                                  in_=y_t[c][:, c0:c1, :].rearrange("p i t -> p (i t)"))
+            nc.sync.dma_start(out=words_out[:, CHUNK * c + c0 : CHUNK * c + c1], in_=y_codes[c][:, c0:c1].bitcast(I32))
+
+        TICKS = 4 * UNITS
+        LF = LR = LT = LY = RADQ = TF = LAG
+        LC = LQ + SP
+        TO = SP
+        last = UNITS - 1
+        n3 = TILES * (CHUNKS - 1)
+        todo = {}
+
+        def at(tick, fn, *args):
+            todo.setdefault(tick, []).append((fn, args))
+
+        for k in range(TICKS):
+            at(k, dots, k // 4, k % 4)
+        at(6, spread_specular)
+        for c in range(CHUNKS - 1):
+            for j in range(TILES):
+                at(12 * c + 12 + LC + SP * j, shade, TILES * c + j, 0, GROUPS)
+            t0 = 12 * c + 12 + LC + 3 * SP + LF + LR + LT
+            at(t0, turn, TILES * c, TILES * c + 2)
+            at(t0, turn, TILES * c + 2, TILES * c + 4)
+        for u in range(last):
+            at(4 * u + 4 + LQ, quantize_lobe, u, 0, CHUNK)
+        for c in range(CHUNKS - 1):
+            for j in range(TILES):
+                at(12 * c + 12 + LC + SP * j + LF, finish, TILES * c + j)
+        for k in range(TICKS):
+            ns = NS0 if k < 16 else NS
+            at(k + LA, relu, k // 4, k % 4, (k * ns) % 12 < ns)
+        for u in range(last):
+            at(4 * u + 4 + LB, square, u, 0, 256)
+            at(4 * u + 6 + LB, square, u, 256, 512)
+        for g in range(1, GROUPS):
+            at(4 * g - 4 + SORT1, sort_lights, g)
+        for g in range(GROUPS):
+            if G_RAD:
+                for h in range(4):
+                    at(RAD0 + RADSTEP * g, interleave_radiance, g, P * h, P * h + P)
+            else:
+                at(RAD0 + RADSTEP * g, interleave_radiance, g, 0, RAD)
+            at(RAD0 + RADSTEP * g + RADQ, quantize_radiance, g)
+        for c in range(CHUNKS - 1):
+            for j in range(TILES):
+                at(12 * c + 12 + LC + SP * j + LF + LR, round_pairs, TILES * c + j, False)
+            t0 = 12 * c + 12 + LC + 3 * SP + LF + LR + LT
+            at(t0 + LG, gather, TILES * c, TILES * c + 2)
+            at(t0 + LG + 1, gather, TILES * c + 2, TILES * c + 4)
+            at(t0 + LG + LY, quantize_result, c, 0, CHUNK)
+        E = TICKS + TE
+        for j in range(TILES):
+            at(TICKS + TO + j, shade, n3 + j, 0, GROUPS - 1)
+            at(TICKS + LB + j, square, last, P * j, P * j + P)
+            at(E + TS * j, quantize_lobe, last, P * j, P * j + P)
+            at(E + TS * j, shade, n3 + j, GROUPS - 1, GROUPS)
+            at(E + TS * j + TF, finish, n3 + j)
+            at(E + TS * j + TF + TR, round_pairs, n3 + j, not G_CAST and j < 3)
+            at(E + TS * j + TF + 1 + TR, turn, n3 + j, n3 + j + 1)
+            at(E + TS * j + TF + 2 + TR, gather, n3 + j, n3 + j + 1)
+            if j % 2:
+                at(E + TS * j + TF + 3 + TR, quantize_result, CHUNKS - 1, P * (j - 1), P * (j + 1))
+
+        sort_lights(0)
+        for tick in sorted(todo):
+            for fn, args in todo[tick]:
+                fn(*args)
+        for q in range(4):
+            queue = nc.scalar if q % 2 else nc.sync
+            queue.dma_start(out=out_2[0].bitcast(I32)[4 * q : 4 * q + 4, :], in_=y_scales[:].bitcast(I32)[32 * q : 32 * q + 4, :])

@@ -26,8 +26,15 @@ UNITS = CHUNKS * GROUPS
 BANKS = 8
 G_CAST = False
 G_RAD = False
-RB = 4
-WARM_S = True
+RB = 8
+RADQ = 3
+LR = 3
+RS = 0
+CS = 48
+BS = 2
+TC = 0
+GP = 4
+WARM_S = False
 LAG = 3
 LA, LB, LQ, LG = 1, 1, 6, 1
 NS = 4
@@ -38,9 +45,14 @@ TE, TS, TR, SP = 4, 1, 2, 2
 
 G_CAST = False
 G_RAD = False
-NS = 4
+NS = 5
 NS0 = 6
-WARM_S = False
+LQ = 5
+TE = 5
+LB = 2
+TC = 3
+RAD0 = 3
+CS = 50
 
 
 def tile_blinn_phong_radiance_features_k5_kernel(
@@ -106,14 +118,14 @@ def tile_blinn_phong_radiance_features_k5_kernel(
             load_scales(nc.sync, hs_raw, half_scales, r, 0, LIGHTS)
         for r in range(4):
             load_scales(nc.sync, as_first, nrm_scales, r, 0, CHUNK)
+        load_radiance(0)
         load_words(nc.sync, hw_raw[1], half_words, 1)
         load_words(nc.sync, hw_raw[2], half_words, 2)
-        load_radiance(0)
         nc.sync.dma_start(out=spec_raw[:], in_=specular.rearrange("(n p) -> n p", p=P))
+        load_radiance(1)
         load_words(nc.sync, aw[1], nrm_words, 1)
         for r in range(4):
             load_scales(nc.sync, as_rest, nrm_scales, r, CHUNK, POINTS - CHUNK)
-        load_radiance(1)
         load_radiance(2)
         load_diffuse(0)
         for c in range(2, CHUNKS):
@@ -126,7 +138,7 @@ def tile_blinn_phong_radiance_features_k5_kernel(
         nc.gpsimd.tensor_copy(out=spec_rows[0:16, :], in_=spec_raw[:])
 
         hw = [kept([P, KP, 4, 256], U8, "hw%d" % g) for g in range(GROUPS)]
-        hs = [kept([P, KP, 4, P], U8, "hs%d" % g) for g in range(GROUPS)]
+        hs = kept([P, GROUPS, KP, 4, P], U8, "hs")
         rad_codes = [kept([P, RAD], U32, "rad_codes%d" % g) for g in range(GROUPS)]
         rad_scales = [kept([P, RAD], U8, "rad_scales%d" % g) for g in range(GROUPS)]
         rad_il = [kept([P, RAD, 4], BF16, "rad_il%d" % g) for g in range(GROUPS)]
@@ -141,16 +153,20 @@ def tile_blinn_phong_radiance_features_k5_kernel(
                 out=hw[g][:].bitcast(I32).rearrange("p k t (j w) -> p k t j w", w=2),
                 in_=hw_raw[g][:].bitcast(I32).rearrange("p k (j t w) -> p k t j w", t=4, w=2),
             )
+
+        def sort_light_scales():
             nc.vector.tensor_copy(
-                out=hs[g][:].bitcast(I32),
-                in_=hs_raw[:].bitcast(I32)[:, :, P * g : P * (g + 1)].rearrange("p k (j t) -> p k t j", t=4),
+                out=hs[:].bitcast(I32),
+                in_=hs_raw[:].bitcast(I32).rearrange("p k (g j t) -> p g k t j", g=GROUPS, t=4),
             )
 
-        def interleave_radiance(g, f0, f1):
+        def interleave_radiance(g, f0, f1, on_scalar):
             dst = rad_il[g][:, f0:f1, :].rearrange("p (c i) t -> p c t i", i=4)
             src = rad_raw[g][:, :, f0:f1].rearrange("p t (c i) -> p c t i", i=4)
             if G_RAD:
                 nc.gpsimd.tensor_scalar(out=rad_il[g][:, f0:f1, :], in0=rad_raw[g][:, :, f0:f1].rearrange("p t f -> p f t"), scalar1=1.0, scalar2=0.0, op0=ALU.mult, op1=ALU.add)
+            elif on_scalar:
+                nc.scalar.copy(out=dst, in_=src)
             else:
                 nc.vector.tensor_copy(out=dst, in_=src)
 
@@ -165,27 +181,34 @@ def tile_blinn_phong_radiance_features_k5_kernel(
 
         def dots(u, t):
             c, g = divmod(u, GROUPS)
+            h, pair = divmod(t, 2)
             bank = next_bank()
             acc["d", u, t] = bank
-            for k in range(KP):
-                a_scale = as_first[:, k, :] if c == 0 else as_rest[:, k, CHUNK * (c - 1) : CHUNK * c]
-                nc.tensor.matmul_mx(out=bank[:], lhsT=hw[g][:, k, t, :].bitcast(FP4X4), lhsT_scale=hs[g][:, k, t, :],
-                                    rhs=aw[c][:, k, :].bitcast(FP4X4), rhs_scale=a_scale, start=(k == 0), stop=(k == KP - 1))
+            for e in range(2):
+                for k in range(KP):
+                    a_scale = as_first[:, k, :] if c == 0 else as_rest[:, k, CHUNK * (c - 1) : CHUNK * c]
+                    nc.tensor.matmul_mx(out=bank[:, 256 * e : 256 * (e + 1)], lhsT=hw[g][:, k, 2 * pair + e, :].bitcast(FP4X4),
+                                        lhsT_scale=hs[:, g, k, 2 * pair + e, :],
+                                        rhs=aw[c][:, k, 512 * h : 512 * (h + 1)].bitcast(FP4X4), rhs_scale=a_scale[:, 256 * h : 256 * (h + 1)],
+                                        start=(k == 0), stop=(k == KP - 1))
 
         def relu(u, t, on_scalar):
-            if t == 0:
-                relu_d[u] = work.tile([P, 4, CHUNK], F32, name="relu%d" % u, tag="relu", bufs=RB)
+            h, pair = divmod(t, 2)
+            if pair == 0:
+                relu_d[u, h] = work.tile([P, 2, 256, 2], F32, name="rel%d_%d" % (u, h), tag="relu", bufs=RB)
+            dst = relu_d[u, h][:, pair, :, :]
+            src = acc["d", u, t][:].rearrange("p (e i) -> p i e", e=2)
             if on_scalar:
-                nc.scalar.activation(out=relu_d[u][:, t, :], in_=acc["d", u, t][:], func=ACT.Relu)
+                nc.scalar.activation(out=dst, in_=src, func=ACT.Relu)
             else:
-                nc.vector.tensor_scalar(out=relu_d[u][:, t, :], in0=acc["d", u, t][:], scalar1=0.0, scalar2=None, op0=ALU.max)
+                nc.vector.tensor_scalar(out=dst, in0=src, scalar1=0.0, scalar2=None, op0=ALU.max)
 
         def square(u, c0, c1):
             if c0 == 0:
                 lobe[u] = work.tile([P, CHUNK, 4], BF16, name="lobe%d" % u, tag="lobe", align_bytes=64)
             cols = slice(c0, c1)
-            nc.scalar.activation(out=lobe[u][:, cols, :].rearrange("p (c i) t -> p c t i", i=2),
-                                 in_=relu_d[u][:, :, cols].rearrange("p t (c i) -> p c t i", i=2), func=ACT.Square)
+            nc.scalar.activation(out=lobe[u][:, cols, :].rearrange("p i (u e) -> p i u e", u=2),
+                                 in_=relu_d[u, c0 // 256][:, :, c0 % 256 : c0 % 256 + c1 - c0, :].rearrange("p u i e -> p i u e"), func=ACT.Square)
 
         def quantize_lobe(u, c0, c1):
             nc.vector.quantize_mx(out=s_codes[u][:, c0:c1].bitcast(FP8X4), scales=s_scales[u][:, c0:c1],
@@ -208,12 +231,12 @@ def tile_blinn_phong_radiance_features_k5_kernel(
                                            op0=ALU.mult, op1=ALU.add)
             nc.sync.dma_start(out=out_0[P * n : P * (n + 1), :], in_=y[n][:])
 
-        def round_pairs(n, on_scalar):
+        def round_pairs(n, on_scalar, on_gpsimd):
             y_pairs[n] = work.tile([P, 2, P, 2], BF16, name="y_pairs%d" % n, tag="y_pairs", bufs=8)
             src = y[n][:].rearrange("p (m u e) -> p u m e", u=2, e=2)
             if on_scalar:
                 nc.scalar.copy(out=y_pairs[n][:], in_=src)
-            elif G_CAST:
+            elif on_gpsimd:
                 nc.gpsimd.tensor_scalar(out=y_pairs[n][:], in0=src, scalar1=1.0, scalar2=0.0, op0=ALU.mult, op1=ALU.add)
             else:
                 nc.vector.tensor_copy(out=y_pairs[n][:], in_=src)
@@ -243,7 +266,7 @@ def tile_blinn_phong_radiance_features_k5_kernel(
             nc.sync.dma_start(out=words_out[:, CHUNK * c + c0 : CHUNK * c + c1], in_=y_codes[c][:, c0:c1].bitcast(I32))
 
         TICKS = 4 * UNITS
-        LF = LR = LT = LY = RADQ = TF = LAG
+        LF = LT = LY = TF = LAG
         LC = LQ + SP
         TO = SP
         last = UNITS - 1
@@ -271,20 +294,26 @@ def tile_blinn_phong_radiance_features_k5_kernel(
             ns = NS0 if k < 16 else NS
             at(k + LA, relu, k // 4, k % 4, (k * ns) % 12 < ns)
         for u in range(last):
-            at(4 * u + 4 + LB, square, u, 0, 256)
-            at(4 * u + 6 + LB, square, u, 256, 512)
+            if BS == 2:
+                at(4 * u + 2 + LB, square, u, 0, 256)
+                at(4 * u + 4 + LB, square, u, 256, 512)
+            else:
+                at(4 * u + 4 + LB, square, u, 0, 512)
         for g in range(1, GROUPS):
             at(4 * g - 4 + SORT1, sort_lights, g)
         for g in range(GROUPS):
             if G_RAD:
-                for h in range(4):
-                    at(RAD0 + RADSTEP * g, interleave_radiance, g, P * h, P * h + P)
+                for h in range(GP):
+                    at(RAD0 + RADSTEP * g, interleave_radiance, g, RAD // GP * h, RAD // GP * (h + 1), False)
             else:
-                at(RAD0 + RADSTEP * g, interleave_radiance, g, 0, RAD)
+                if RS < RAD:
+                    at(RAD0 + RADSTEP * g, interleave_radiance, g, RS, RAD, False)
+                if RS:
+                    at(RAD0 + RADSTEP * g, interleave_radiance, g, 0, RS, True)
             at(RAD0 + RADSTEP * g + RADQ, quantize_radiance, g)
         for c in range(CHUNKS - 1):
             for j in range(TILES):
-                at(12 * c + 12 + LC + SP * j + LF + LR, round_pairs, TILES * c + j, False)
+                at(12 * c + 12 + LC + SP * j + LF + LR, round_pairs, TILES * c + j, 12 * c + 12 + LC + SP * j + LF + LR >= CS, G_CAST)
             t0 = 12 * c + 12 + LC + 3 * SP + LF + LR + LT
             at(t0 + LG, gather, TILES * c, TILES * c + 2)
             at(t0 + LG + 1, gather, TILES * c + 2, TILES * c + 4)
@@ -292,17 +321,18 @@ def tile_blinn_phong_radiance_features_k5_kernel(
         E = TICKS + TE
         for j in range(TILES):
             at(TICKS + TO + j, shade, n3 + j, 0, GROUPS - 1)
-            at(TICKS + LB + j, square, last, P * j, P * j + P)
+            at(TICKS - 2 + LB + j, square, last, P * j, P * j + P)
             at(E + TS * j, quantize_lobe, last, P * j, P * j + P)
             at(E + TS * j, shade, n3 + j, GROUPS - 1, GROUPS)
             at(E + TS * j + TF, finish, n3 + j)
-            at(E + TS * j + TF + TR, round_pairs, n3 + j, not G_CAST and j < 3)
+            at(E + TS * j + TF + TR, round_pairs, n3 + j, j >= TC and j < 3, G_CAST and j < TC)
             at(E + TS * j + TF + 1 + TR, turn, n3 + j, n3 + j + 1)
             at(E + TS * j + TF + 2 + TR, gather, n3 + j, n3 + j + 1)
             if j % 2:
                 at(E + TS * j + TF + 3 + TR, quantize_result, CHUNKS - 1, P * (j - 1), P * (j + 1))
 
         sort_lights(0)
+        sort_light_scales()
         for tick in sorted(todo):
             for fn, args in todo[tick]:
                 fn(*args)

@@ -17,42 +17,27 @@ ACT = mybir.ActivationFunctionType
 ALU = mybir.AluOpType
 
 P = 128
+SLOTS = 4
+K_PASS = P * SLOTS
+PASSES = FEATS // K_PASS
+GROUPS = LIGHTS // K_PASS
 CHUNK = 512
+HALF = CHUNK // 2
 CHUNKS = POINTS // CHUNK
-GROUPS = LIGHTS // 512
-KP = FEATS // 512
 TILES = CHUNK // P
 UNITS = CHUNKS * GROUPS
 BANKS = 8
-G_CAST = False
-G_RAD = False
-RB = 8
-RADQ = 3
-LR = 3
-RS = 0
-CS = 48
-BS = 2
-TC = 0
-GP = 4
-WARM_S = False
-LAG = 3
-LA, LB, LQ, LG = 1, 1, 6, 1
-NS = 4
-NS0 = 6
-RAD0, RADSTEP = 5, 4
-SORT1 = 1
-TE, TS, TR, SP = 4, 1, 2, 2
+RAD_PIECES = 4
 
-G_CAST = False
-G_RAD = False
-NS = 5
-NS0 = 6
-LQ = 5
-TE = 5
-LB = 2
-TC = 3
-RAD0 = 3
-CS = 50
+UNIT_TICKS = 4
+CHUNK_TICKS = UNIT_TICKS * GROUPS
+TICKS = UNIT_TICKS * UNITS
+SCALAR_EVERY = 3
+LAG = 3
+QUANT_LAG = 5
+SHADE_STEP = 2
+RAD_STEP = 6
+WARM_PASSES = 18
 
 
 def tile_blinn_phong_radiance_features_k5_kernel(
@@ -75,100 +60,105 @@ def tile_blinn_phong_radiance_features_k5_kernel(
         def kept(shape, dtype, name):
             return keep.tile(shape, dtype, name=name, align_bytes=64)
 
-        hw_raw = [kept([P, KP, 1024], U8, "hw_raw%d" % g) for g in range(GROUPS)]
-        hs_raw = kept([P, KP, LIGHTS], U8, "hs_raw")
-        aw = [kept([P, KP, 2 * CHUNK], U8, "aw%d" % c) for c in range(CHUNKS)]
-        as_first = kept([P, KP, CHUNK], U8, "as_first")
-        as_rest = kept([P, KP, POINTS - CHUNK], U8, "as_rest")
-        rad_raw = [kept([P, 4, RAD], BF16, "rad_raw%d" % g) for g in range(GROUPS)]
+        hw_raw = [kept([P, PASSES, 2 * K_PASS], U8, "hw_raw%d" % g) for g in range(GROUPS)]
+        hs_raw = kept([P, PASSES, LIGHTS], U8, "hs_raw")
+        aw = [kept([P, PASSES, 2 * CHUNK], U8, "aw%d" % c) for c in range(CHUNKS)]
+        as_first = kept([P, PASSES, CHUNK], U8, "as_first")
+        as_rest = kept([P, PASSES, POINTS - CHUNK], U8, "as_rest")
+        rad_raw = [kept([P, SLOTS, RAD], BF16, "rad_raw%d" % g) for g in range(GROUPS)]
         dif = [kept([P, TILES, RAD], BF16, "dif%d" % c) for c in range(CHUNKS)]
-        spec_raw = kept([16, P], BF16, "spec_raw")
+        spec_raw = kept([POINTS // P, P], BF16, "spec_raw")
         spec_rows = kept([P, P], F32, "spec_rows")
-        spec = kept([P, 16], F32, "spec")
+        spec = kept([P, POINTS // P], F32, "spec")
         ident = kept([P, P], F32, "ident")
-        warm = kept([P, 8], F32, "warm")
-        warm2 = kept([P, 8], F32, "warm2")
 
-        def load_words(queue, dst, words, block):
+        def load_words(dst, words, block):
             src = words.bitcast(I32)[:, :, 256 * block : 256 * (block + 1)]
-            queue.dma_start(out=dst[:].bitcast(I32), in_=src.rearrange("k p w -> p k w"))
+            nc.sync.dma_start(out=dst[:].bitcast(I32), in_=src.rearrange("k p w -> p k w"))
 
-        def load_scales(queue, dst, scales, r, col0, cols):
-            src = scales.bitcast(I32).rearrange("k (q r) w -> r q k w", r=4)[r]
-            queue.dma_start(out=dst[:].bitcast(I32)[r:P:32], in_=src[:, :, col0 // 4 : (col0 + cols) // 4])
+        def load_scales(dst, scales, col0, cols):
+            for r in range(4):
+                src = scales.bitcast(I32).rearrange("k (q r) w -> r q k w", r=4)[r]
+                nc.sync.dma_start(out=dst[:].bitcast(I32)[r:P:32], in_=src[:, :, col0 // 4 : (col0 + cols) // 4])
 
         def load_radiance(g):
-            src = radiance[512 * g : 512 * (g + 1), :].rearrange("(j t b) f -> b j t f", t=4, b=4)
+            src = radiance[K_PASS * g : K_PASS * (g + 1), :].rearrange("(j t b) f -> b j t f", t=SLOTS, b=4)
             for b in range(4):
                 nc.sync.dma_start(out=rad_raw[g][b:P:4], in_=src[b])
 
         def load_diffuse(c):
-            nc.sync.dma_start(out=dif[c][:], in_=diffuse[CHUNK * c : CHUNK * (c + 1), :].rearrange("(j p) f -> p j f", p=P))
+            src = diffuse[CHUNK * c : CHUNK * (c + 1), :].rearrange("(j p) f -> p j f", p=P)
+            nc.sync.dma_start(out=dif[c][:], in_=src)
 
+        zeros = kept([P, K_PASS], BF16, "zeros")
+        zero_codes = kept([P, P], U32, "zero_codes")
+        zero_scales = kept([P, P], U8, "zero_scales")
         nc.vector.memset(hs_raw[:].bitcast(I32), 0)
         nc.vector.memset(as_first[:].bitcast(I32), 0)
-        if WARM_S:
-            nc.vector.memset(warm[:], 0.0)
+        nc.vector.memset(zeros[:], 0.0)
         nc.vector.memset(as_rest[:].bitcast(I32), 0)
-        if WARM_S:
-            nc.scalar.activation(out=warm2[:], in_=warm[:], func=ACT.Square)
-        load_words(nc.sync, hw_raw[0], half_words, 0)
-        load_words(nc.sync, aw[0], nrm_words, 0)
-        for r in range(4):
-            load_scales(nc.sync, hs_raw, half_scales, r, 0, LIGHTS)
-        for r in range(4):
-            load_scales(nc.sync, as_first, nrm_scales, r, 0, CHUNK)
+
+        nc.vector.quantize_mx(out=zero_codes[:].bitcast(FP8X4), scales=zero_scales[:], in_=zeros[:])
+        warm_bank = next_bank()
+        for warm_pass in range(WARM_PASSES):
+            nc.tensor.matmul_mx(out=warm_bank[:, 0:P], lhsT=zero_codes[:].bitcast(FP8X4), lhsT_scale=zero_scales[:],
+                                rhs=zero_codes[:].bitcast(FP8X4), rhs_scale=zero_scales[:], start=True, stop=True)
+
+        load_words(hw_raw[0], half_words, 0)
+        load_words(aw[0], nrm_words, 0)
+        load_scales(hs_raw, half_scales, 0, LIGHTS)
+        load_scales(as_first, nrm_scales, 0, CHUNK)
+        load_words(hw_raw[1], half_words, 1)
         load_radiance(0)
-        load_words(nc.sync, hw_raw[1], half_words, 1)
-        load_words(nc.sync, hw_raw[2], half_words, 2)
+        load_words(hw_raw[2], half_words, 2)
         nc.sync.dma_start(out=spec_raw[:], in_=specular.rearrange("(n p) -> n p", p=P))
         load_radiance(1)
-        load_words(nc.sync, aw[1], nrm_words, 1)
-        for r in range(4):
-            load_scales(nc.sync, as_rest, nrm_scales, r, CHUNK, POINTS - CHUNK)
+        load_words(aw[1], nrm_words, 1)
+        load_scales(as_rest, nrm_scales, CHUNK, POINTS - CHUNK)
         load_radiance(2)
         load_diffuse(0)
         for c in range(2, CHUNKS):
-            load_words(nc.sync, aw[c], nrm_words, c)
+            load_words(aw[c], nrm_words, c)
         for c in range(1, CHUNKS):
             load_diffuse(c)
 
         make_identity(nc, ident[:])
         nc.gpsimd.memset(spec_rows[:], 0.0)
-        nc.gpsimd.tensor_copy(out=spec_rows[0:16, :], in_=spec_raw[:])
+        nc.gpsimd.tensor_copy(out=spec_rows[0 : POINTS // P, :], in_=spec_raw[:])
 
-        hw = [kept([P, KP, 4, 256], U8, "hw%d" % g) for g in range(GROUPS)]
-        hs = kept([P, GROUPS, KP, 4, P], U8, "hs")
+        hw = [kept([P, PASSES, SLOTS, 2 * P], U8, "hw%d" % g) for g in range(GROUPS)]
+        hs = kept([P, GROUPS, PASSES, SLOTS, P], U8, "hs")
         rad_codes = [kept([P, RAD], U32, "rad_codes%d" % g) for g in range(GROUPS)]
         rad_scales = [kept([P, RAD], U8, "rad_scales%d" % g) for g in range(GROUPS)]
-        rad_il = [kept([P, RAD, 4], BF16, "rad_il%d" % g) for g in range(GROUPS)]
+        rad_il = [kept([P, RAD, SLOTS], BF16, "rad_il%d" % g) for g in range(GROUPS)]
         s_codes = [kept([P, CHUNK], U32, "s_codes%d" % u) for u in range(UNITS)]
         s_scales = [kept([P, CHUNK], U8, "s_scales%d" % u) for u in range(UNITS)]
         y_codes = [kept([P, CHUNK], U32, "y_codes%d" % c) for c in range(CHUNKS)]
         y_scales = kept([P, POINTS], U8, "y_scales")
-        relu_d, lobe, acc, y, y_pairs, turned, y_t = {}, {}, {}, {}, {}, {}, {}
+        d_bank, c_bank, turned, relu_d, lobe, y, y_pairs, y_t = {}, {}, {}, {}, {}, {}, {}, {}
+        words_out = out_1[0].rearrange("p m t -> p (m t)").bitcast(I32)
 
         def sort_lights(g):
             nc.vector.tensor_copy(
                 out=hw[g][:].bitcast(I32).rearrange("p k t (j w) -> p k t j w", w=2),
-                in_=hw_raw[g][:].bitcast(I32).rearrange("p k (j t w) -> p k t j w", t=4, w=2),
+                in_=hw_raw[g][:].bitcast(I32).rearrange("p k (j t w) -> p k t j w", t=SLOTS, w=2),
             )
 
         def sort_light_scales():
             nc.vector.tensor_copy(
                 out=hs[:].bitcast(I32),
-                in_=hs_raw[:].bitcast(I32).rearrange("p k (g j t) -> p g k t j", g=GROUPS, t=4),
+                in_=hs_raw[:].bitcast(I32).rearrange("p k (g j t) -> p g k t j", g=GROUPS, t=SLOTS),
             )
 
-        def interleave_radiance(g, f0, f1, on_scalar):
-            dst = rad_il[g][:, f0:f1, :].rearrange("p (c i) t -> p c t i", i=4)
-            src = rad_raw[g][:, :, f0:f1].rearrange("p t (c i) -> p c t i", i=4)
-            if G_RAD:
-                nc.gpsimd.tensor_scalar(out=rad_il[g][:, f0:f1, :], in0=rad_raw[g][:, :, f0:f1].rearrange("p t f -> p f t"), scalar1=1.0, scalar2=0.0, op0=ALU.mult, op1=ALU.add)
-            elif on_scalar:
-                nc.scalar.copy(out=dst, in_=src)
-            else:
-                nc.vector.tensor_copy(out=dst, in_=src)
+        def interleave_first_radiance():
+            nc.vector.tensor_copy(out=rad_il[0][:].rearrange("p (c i) t -> p c t i", i=4),
+                                  in_=rad_raw[0][:].rearrange("p t (c i) -> p c t i", i=4))
+
+        def interleave_radiance(g):
+            for piece in range(RAD_PIECES):
+                cols = slice(RAD // RAD_PIECES * piece, RAD // RAD_PIECES * (piece + 1))
+                nc.gpsimd.tensor_scalar(out=rad_il[g][:, cols, :], in0=rad_raw[g][:, :, cols].rearrange("p t f -> p f t"),
+                                        scalar1=1.0, scalar2=0.0, op0=ALU.mult, op1=ALU.add)
 
         def quantize_radiance(g):
             nc.vector.quantize_mx(out=rad_codes[g][:].bitcast(FP8X4), scales=rad_scales[g][:],
@@ -177,38 +167,42 @@ def tile_blinn_phong_radiance_features_k5_kernel(
         def spread_specular():
             bank = next_bank()
             nc.tensor.transpose(bank[:, 0:P], spec_rows[:], ident[:])
-            nc.scalar.copy(out=spec[:], in_=bank[:, 0:16])
+            nc.scalar.copy(out=spec[:], in_=bank[:, 0 : POINTS // P])
 
-        def dots(u, t):
+        def dots(tick):
+            u, step = divmod(tick, UNIT_TICKS)
             c, g = divmod(u, GROUPS)
-            h, pair = divmod(t, 2)
-            bank = next_bank()
-            acc["d", u, t] = bank
+            h, pair = divmod(step, 2)
+            d_bank[tick] = next_bank()
             for e in range(2):
-                for k in range(KP):
+                for k in range(PASSES):
                     a_scale = as_first[:, k, :] if c == 0 else as_rest[:, k, CHUNK * (c - 1) : CHUNK * c]
-                    nc.tensor.matmul_mx(out=bank[:, 256 * e : 256 * (e + 1)], lhsT=hw[g][:, k, 2 * pair + e, :].bitcast(FP4X4),
-                                        lhsT_scale=hs[:, g, k, 2 * pair + e, :],
-                                        rhs=aw[c][:, k, 512 * h : 512 * (h + 1)].bitcast(FP4X4), rhs_scale=a_scale[:, 256 * h : 256 * (h + 1)],
-                                        start=(k == 0), stop=(k == KP - 1))
+                    nc.tensor.matmul_mx(
+                        out=d_bank[tick][:, HALF * e : HALF * (e + 1)],
+                        lhsT=hw[g][:, k, 2 * pair + e, :].bitcast(FP4X4), lhsT_scale=hs[:, g, k, 2 * pair + e, :],
+                        rhs=aw[c][:, k, 2 * HALF * h : 2 * HALF * (h + 1)].bitcast(FP4X4),
+                        rhs_scale=a_scale[:, HALF * h : HALF * (h + 1)],
+                        start=(k == 0), stop=(k == PASSES - 1))
 
-        def relu(u, t, on_scalar):
-            h, pair = divmod(t, 2)
+        def relu(tick):
+            u, step = divmod(tick, UNIT_TICKS)
+            h, pair = divmod(step, 2)
             if pair == 0:
-                relu_d[u, h] = work.tile([P, 2, 256, 2], F32, name="rel%d_%d" % (u, h), tag="relu", bufs=RB)
+                relu_d[u, h] = work.tile([P, 2, HALF, 2], F32, name="rel%d_%d" % (u, h), tag="relu", bufs=8)
             dst = relu_d[u, h][:, pair, :, :]
-            src = acc["d", u, t][:].rearrange("p (e i) -> p i e", e=2)
-            if on_scalar:
+            src = d_bank[tick][:].rearrange("p (e i) -> p i e", e=2)
+            if tick % SCALAR_EVERY == 0:
                 nc.scalar.activation(out=dst, in_=src, func=ACT.Relu)
             else:
                 nc.vector.tensor_scalar(out=dst, in0=src, scalar1=0.0, scalar2=None, op0=ALU.max)
 
         def square(u, c0, c1):
             if c0 == 0:
-                lobe[u] = work.tile([P, CHUNK, 4], BF16, name="lobe%d" % u, tag="lobe", align_bytes=64)
-            cols = slice(c0, c1)
-            nc.scalar.activation(out=lobe[u][:, cols, :].rearrange("p i (u e) -> p i u e", u=2),
-                                 in_=relu_d[u, c0 // 256][:, :, c0 % 256 : c0 % 256 + c1 - c0, :].rearrange("p u i e -> p i u e"), func=ACT.Square)
+                lobe[u] = work.tile([P, CHUNK, SLOTS], BF16, name="lobe%d" % u, tag="lobe", align_bytes=64)
+            h, first = divmod(c0, HALF)
+            nc.scalar.activation(out=lobe[u][:, c0:c1, :].rearrange("p i (u e) -> p i u e", u=2),
+                                 in_=relu_d[u, h][:, :, first : first + c1 - c0, :].rearrange("p u i e -> p i u e"),
+                                 func=ACT.Square)
 
         def quantize_lobe(u, c0, c1):
             nc.vector.quantize_mx(out=s_codes[u][:, c0:c1].bitcast(FP8X4), scales=s_scales[u][:, c0:c1],
@@ -217,125 +211,148 @@ def tile_blinn_phong_radiance_features_k5_kernel(
         def shade(n, g0, g1):
             c, j = divmod(n, TILES)
             if g0 == 0:
-                acc["c", n] = next_bank()
+                c_bank[n] = next_bank()
             cols = slice(P * j, P * (j + 1))
             for g in range(g0, g1):
                 u = GROUPS * c + g
-                nc.tensor.matmul_mx(out=acc["c", n][:], lhsT=s_codes[u][:, cols].bitcast(FP8X4), lhsT_scale=s_scales[u][:, cols],
-                                    rhs=rad_codes[g][:].bitcast(FP8X4), rhs_scale=rad_scales[g][:], start=(g == 0), stop=(g == GROUPS - 1))
+                nc.tensor.matmul_mx(out=c_bank[n][:], lhsT=s_codes[u][:, cols].bitcast(FP8X4), lhsT_scale=s_scales[u][:, cols],
+                                    rhs=rad_codes[g][:].bitcast(FP8X4), rhs_scale=rad_scales[g][:],
+                                    start=(g == 0), stop=(g == GROUPS - 1))
 
         def finish(n):
             c, j = divmod(n, TILES)
             y[n] = work.tile([P, RAD], F32, name="y%d" % n, tag="y", bufs=6)
-            nc.vector.scalar_tensor_tensor(out=y[n][:], in0=acc["c", n][:], scalar=spec[:, n : n + 1], in1=dif[c][:, j, :],
+            nc.vector.scalar_tensor_tensor(out=y[n][:], in0=c_bank[n][:], scalar=spec[:, n : n + 1], in1=dif[c][:, j, :],
                                            op0=ALU.mult, op1=ALU.add)
             nc.sync.dma_start(out=out_0[P * n : P * (n + 1), :], in_=y[n][:])
 
-        def round_pairs(n, on_scalar, on_gpsimd):
+        def round_pairs(n):
             y_pairs[n] = work.tile([P, 2, P, 2], BF16, name="y_pairs%d" % n, tag="y_pairs", bufs=8)
             src = y[n][:].rearrange("p (m u e) -> p u m e", u=2, e=2)
-            if on_scalar:
-                nc.scalar.copy(out=y_pairs[n][:], in_=src)
-            elif on_gpsimd:
-                nc.gpsimd.tensor_scalar(out=y_pairs[n][:], in0=src, scalar1=1.0, scalar2=0.0, op0=ALU.mult, op1=ALU.add)
-            else:
+            if n == TILES * CHUNKS - 1:
                 nc.vector.tensor_copy(out=y_pairs[n][:], in_=src)
+            elif n == TILES * CHUNKS - 2:
+                nc.scalar.copy(out=y_pairs[n][:], in_=src)
+            else:
+                nc.gpsimd.tensor_scalar(out=y_pairs[n][:], in0=src, scalar1=1.0, scalar2=0.0, op0=ALU.mult, op1=ALU.add)
 
-        def turn(n0, n1):
-            bank = next_bank()
-            turned[n0] = bank
-            for n in range(n0, n1):
-                words = y_pairs[n][:].rearrange("p u m e -> p u (m e)").bitcast(F32)
+        def turn(n0):
+            turned[n0] = next_bank()
+            for s in range(2):
+                words = y_pairs[n0 + s][:].rearrange("p u m e -> p u (m e)").bitcast(F32)
                 for u in range(2):
-                    col = P * (2 * (n - n0) + u)
-                    nc.tensor.transpose(bank[:, col : col + P], words[:, u, :], ident[:])
+                    col = P * (2 * s + u)
+                    nc.tensor.transpose(turned[n0][:, col : col + P], words[:, u, :], ident[:])
 
-        def gather(n0, n1):
+        def gather(n0):
             c, j = divmod(n0, TILES)
             if j == 0:
-                y_t[c] = work.tile([P, CHUNK, 4], BF16, name="y_t%d" % c, tag="y_t", bufs=2, align_bytes=64)
-            s = n1 - n0
-            dst = y_t[c][:, P * j : P * (j + s), :].bitcast(F32).rearrange("p (s i) u -> p s i u", s=s)
-            nc.scalar.copy(out=dst, in_=turned[n0][:, 0 : 2 * P * s].rearrange("p (s u i) -> p s i u", s=s, u=2))
-
-        words_out = out_1[0].rearrange("p m t -> p (m t)").bitcast(I32)
+                y_t[c] = work.tile([P, CHUNK, SLOTS], BF16, name="y_t%d" % c, tag="y_t", align_bytes=64)
+            dst = y_t[c][:, P * j : P * (j + 2), :].bitcast(F32).rearrange("p (s i) u -> p s i u", s=2)
+            nc.scalar.copy(out=dst, in_=turned[n0][:].rearrange("p (s u i) -> p s i u", s=2, u=2))
 
         def quantize_result(c, c0, c1):
-            nc.vector.quantize_mx(out=y_codes[c][:, c0:c1].bitcast(FP8X4), scales=y_scales[:, CHUNK * c + c0 : CHUNK * c + c1],
+            cols = slice(CHUNK * c + c0, CHUNK * c + c1)
+            nc.vector.quantize_mx(out=y_codes[c][:, c0:c1].bitcast(FP8X4), scales=y_scales[:, cols],
                                   in_=y_t[c][:, c0:c1, :].rearrange("p i t -> p (i t)"))
-            nc.sync.dma_start(out=words_out[:, CHUNK * c + c0 : CHUNK * c + c1], in_=y_codes[c][:, c0:c1].bitcast(I32))
+            nc.sync.dma_start(out=words_out[:, cols], in_=y_codes[c][:, c0:c1].bitcast(I32))
 
-        TICKS = 4 * UNITS
-        LF = LT = LY = TF = LAG
-        LC = LQ + SP
-        TO = SP
+        steps = {}
+
+        def at(tick, step, *args):
+            if tick < TICKS:
+                steps.setdefault(tick, []).append((step, args))
+
+        def quant_tick(u):
+            return UNIT_TICKS * (u + 1) + QUANT_LAG
+
+        def shade_tick(n):
+            c, j = divmod(n, TILES)
+            put_off = CHUNK_TICKS - TILES * SHADE_STEP if c == 0 else 0
+            return quant_tick(GROUPS * c + GROUPS - 1) + SHADE_STEP * (j + 1) + put_off
+
+        def turn_tick(c):
+            return shade_tick(TILES * c + TILES - 1) + 3 * LAG
+
         last = UNITS - 1
-        n3 = TILES * (CHUNKS - 1)
-        todo = {}
-
-        def at(tick, fn, *args):
-            todo.setdefault(tick, []).append((fn, args))
-
-        for k in range(TICKS):
-            at(k, dots, k // 4, k % 4)
-        at(6, spread_specular)
+        tail = TILES * (CHUNKS - 1)
+        for tick in range(TICKS):
+            at(tick, dots, tick)
+        at(CHUNK_TICKS, spread_specular)
         for c in range(CHUNKS - 1):
-            for j in range(TILES):
-                at(12 * c + 12 + LC + SP * j, shade, TILES * c + j, 0, GROUPS)
-            t0 = 12 * c + 12 + LC + 3 * SP + LF + LR + LT
-            at(t0, turn, TILES * c, TILES * c + 2)
-            at(t0, turn, TILES * c + 2, TILES * c + 4)
+            for n in range(TILES * c, TILES * (c + 1)):
+                at(shade_tick(n), shade, n, 0, GROUPS)
+            at(turn_tick(c), turn, TILES * c)
+            at(turn_tick(c), turn, TILES * c + 2)
         for u in range(last):
-            at(4 * u + 4 + LQ, quantize_lobe, u, 0, CHUNK)
-        for c in range(CHUNKS - 1):
-            for j in range(TILES):
-                at(12 * c + 12 + LC + SP * j + LF, finish, TILES * c + j)
-        for k in range(TICKS):
-            ns = NS0 if k < 16 else NS
-            at(k + LA, relu, k // 4, k % 4, (k * ns) % 12 < ns)
+            at(quant_tick(u), quantize_lobe, u, 0, CHUNK)
+        for n in range(tail):
+            at(shade_tick(n) + LAG, finish, n)
+        for tick in range(TICKS):
+            at(tick + 1, relu, tick)
         for u in range(last):
-            if BS == 2:
-                at(4 * u + 2 + LB, square, u, 0, 256)
-                at(4 * u + 4 + LB, square, u, 256, 512)
-            else:
-                at(4 * u + 4 + LB, square, u, 0, 512)
-        for g in range(1, GROUPS):
-            at(4 * g - 4 + SORT1, sort_lights, g)
+            at(UNIT_TICKS * u + 4, square, u, 0, HALF)
+            at(UNIT_TICKS * u + 6, square, u, HALF, CHUNK)
+        at(0, sort_lights, 1)
+        at(UNIT_TICKS + 1, sort_lights, 2)
+        at(2, interleave_first_radiance)
         for g in range(GROUPS):
-            if G_RAD:
-                for h in range(GP):
-                    at(RAD0 + RADSTEP * g, interleave_radiance, g, RAD // GP * h, RAD // GP * (h + 1), False)
-            else:
-                if RS < RAD:
-                    at(RAD0 + RADSTEP * g, interleave_radiance, g, RS, RAD, False)
-                if RS:
-                    at(RAD0 + RADSTEP * g, interleave_radiance, g, 0, RS, True)
-            at(RAD0 + RADSTEP * g + RADQ, quantize_radiance, g)
+            if g > 0:
+                at(2 + RAD_STEP * (g - 1) + LAG, interleave_radiance, g)
+            at(2 + RAD_STEP * g + LAG, quantize_radiance, g)
         for c in range(CHUNKS - 1):
-            for j in range(TILES):
-                at(12 * c + 12 + LC + SP * j + LF + LR, round_pairs, TILES * c + j, 12 * c + 12 + LC + SP * j + LF + LR >= CS, G_CAST)
-            t0 = 12 * c + 12 + LC + 3 * SP + LF + LR + LT
-            at(t0 + LG, gather, TILES * c, TILES * c + 2)
-            at(t0 + LG + 1, gather, TILES * c + 2, TILES * c + 4)
-            at(t0 + LG + LY, quantize_result, c, 0, CHUNK)
-        E = TICKS + TE
-        for j in range(TILES):
-            at(TICKS + TO + j, shade, n3 + j, 0, GROUPS - 1)
-            at(TICKS - 2 + LB + j, square, last, P * j, P * j + P)
-            at(E + TS * j, quantize_lobe, last, P * j, P * j + P)
-            at(E + TS * j, shade, n3 + j, GROUPS - 1, GROUPS)
-            at(E + TS * j + TF, finish, n3 + j)
-            at(E + TS * j + TF + TR, round_pairs, n3 + j, j >= TC and j < 3, G_CAST and j < TC)
-            at(E + TS * j + TF + 1 + TR, turn, n3 + j, n3 + j + 1)
-            at(E + TS * j + TF + 2 + TR, gather, n3 + j, n3 + j + 1)
-            if j % 2:
-                at(E + TS * j + TF + 3 + TR, quantize_result, CHUNKS - 1, P * (j - 1), P * (j + 1))
+            for n in range(TILES * c, TILES * (c + 1)):
+                at(shade_tick(n) + 2 * LAG, round_pairs, n)
+            at(turn_tick(c) + 1, gather, TILES * c)
+            at(turn_tick(c) + 2, gather, TILES * c + 2)
+            at(turn_tick(c) + 1 + LAG, quantize_result, c, 0, CHUNK)
+        at(TICKS - 1, square, last, 0, P)
+        at(TICKS - 1, square, last, P, HALF)
 
         sort_lights(0)
         sort_light_scales()
-        for tick in sorted(todo):
-            for fn, args in todo[tick]:
-                fn(*args)
+        for tick in range(TICKS):
+            for step, args in steps[tick]:
+                step(*args)
+
+        relu(TICKS - 1)
+        shade(tail - 1, 0, GROUPS)
+        square(last, HALF, HALF + P)
+        square(last, HALF + P, CHUNK)
+        quantize_lobe(last - 1, 0, CHUNK)
+        finish(tail - 3)
+        round_pairs(tail - 4)
+        gather(tail - TILES - 2)
+        shade(tail, 0, GROUPS - 1)
+        shade(tail + 1, 0, GROUPS - 1)
+        quantize_lobe(last, 0, HALF)
+        finish(tail - 2)
+        round_pairs(tail - 3)
+        shade(tail, GROUPS - 1, GROUPS)
+        shade(tail + 1, GROUPS - 1, GROUPS)
+        quantize_lobe(last, HALF, CHUNK)
+        finish(tail - 1)
+        round_pairs(tail - 2)
+        shade(tail + 2, 0, GROUPS)
+        shade(tail + 3, 0, GROUPS)
+        round_pairs(tail - 1)
+        for n0 in (tail - 4, tail - 2):
+            turn(n0)
+        for n0 in (tail - 4, tail - 2):
+            gather(n0)
+        for n in range(tail, tail + TILES - 1):
+            finish(n)
+            round_pairs(n)
+        turn(tail)
+        gather(tail)
+        finish(tail + 3)
+        round_pairs(tail + 3)
+        turn(tail + 2)
+        quantize_result(CHUNKS - 3, 0, CHUNK)
+        gather(tail + 2)
+        quantize_result(CHUNKS - 2, 0, CHUNK)
+        quantize_result(CHUNKS - 1, 0, HALF)
+        quantize_result(CHUNKS - 1, HALF, CHUNK)
         for q in range(4):
             queue = nc.scalar if q % 2 else nc.sync
             queue.dma_start(out=out_2[0].bitcast(I32)[4 * q : 4 * q + 4, :], in_=y_scales[:].bitcast(I32)[32 * q : 32 * q + 4, :])

@@ -27,16 +27,16 @@ CHUNKS = POINTS // CHUNK
 TILES = CHUNK // P
 UNITS = CHUNKS * GROUPS
 BANKS = 8
-RAD_PIECES = 4
 
 UNIT_TICKS = 4
 CHUNK_TICKS = UNIT_TICKS * GROUPS
 TICKS = UNIT_TICKS * UNITS
 SCALAR_EVERY = 3
+PREPARE_TICKS = UNIT_TICKS * (GROUPS + 1)
 LAG = 3
 QUANT_LAG = 5
 SHADE_STEP = 2
-RAD_STEP = 6
+RAD_STEP = 5
 WARM_PASSES = 18
 
 
@@ -150,15 +150,9 @@ def tile_blinn_phong_radiance_features_k5_kernel(
                 in_=hs_raw[:].bitcast(I32).rearrange("p k (g j t) -> p g k t j", g=GROUPS, t=SLOTS),
             )
 
-        def interleave_first_radiance():
-            nc.vector.tensor_copy(out=rad_il[0][:].rearrange("p (c i) t -> p c t i", i=4),
-                                  in_=rad_raw[0][:].rearrange("p t (c i) -> p c t i", i=4))
-
         def interleave_radiance(g):
-            for piece in range(RAD_PIECES):
-                cols = slice(RAD // RAD_PIECES * piece, RAD // RAD_PIECES * (piece + 1))
-                nc.gpsimd.tensor_scalar(out=rad_il[g][:, cols, :], in0=rad_raw[g][:, :, cols].rearrange("p t f -> p f t"),
-                                        scalar1=1.0, scalar2=0.0, op0=ALU.mult, op1=ALU.add)
+            nc.vector.tensor_copy(out=rad_il[g][:].rearrange("p (c i) t -> p c t i", i=4),
+                                  in_=rad_raw[g][:].rearrange("p t (c i) -> p c t i", i=4))
 
         def quantize_radiance(g):
             nc.vector.quantize_mx(out=rad_codes[g][:].bitcast(FP8X4), scales=rad_scales[g][:],
@@ -191,7 +185,7 @@ def tile_blinn_phong_radiance_features_k5_kernel(
                 relu_d[u, h] = work.tile([P, 2, HALF, 2], F32, name="rel%d_%d" % (u, h), tag="relu", bufs=8)
             dst = relu_d[u, h][:, pair, :, :]
             src = d_bank[tick][:].rearrange("p (e i) -> p i e", e=2)
-            if tick % SCALAR_EVERY == 0:
+            if tick % (2 if tick < PREPARE_TICKS else SCALAR_EVERY) == 0:
                 nc.scalar.activation(out=dst, in_=src, func=ACT.Relu)
             else:
                 nc.vector.tensor_scalar(out=dst, in0=src, scalar1=0.0, scalar2=None, op0=ALU.max)
@@ -295,10 +289,8 @@ def tile_blinn_phong_radiance_features_k5_kernel(
             at(UNIT_TICKS * u + 6, square, u, HALF, CHUNK)
         at(0, sort_lights, 1)
         at(UNIT_TICKS + 1, sort_lights, 2)
-        at(2, interleave_first_radiance)
         for g in range(GROUPS):
-            if g > 0:
-                at(2 + RAD_STEP * (g - 1) + LAG, interleave_radiance, g)
+            at(2 + RAD_STEP * g, interleave_radiance, g)
             at(2 + RAD_STEP * g + LAG, quantize_radiance, g)
         for c in range(CHUNKS - 1):
             for n in range(TILES * c, TILES * (c + 1)):

from contextlib import ExitStack

import concourse.mybir as mybir
from concourse.masks import make_identity

POINTS, FEATS, LIGHTS, RAD = 2048, 1024, 1536, 512
FLOPS = 2 * POINTS * FEATS * LIGHTS + 2 * POINTS * LIGHTS * RAD

F32 = mybir.dt.float32
BF16 = mybir.dt.bfloat16
I32 = mybir.dt.int32
U32 = mybir.dt.uint32
U8 = mybir.dt.uint8
FP8X4 = mybir.dt.float8_e4m3fn_x4
FP4X4 = mybir.dt.float4_e2m1fn_x4
ACT = mybir.ActivationFunctionType
ALU = mybir.AluOpType

P = 128
SLOTS = 4
K_PASS = P * SLOTS
PASSES = FEATS // K_PASS
GROUPS = LIGHTS // K_PASS
CHUNK = 512
HALF = CHUNK // 2
CHUNKS = POINTS // CHUNK
TILES = CHUNK // P
UNITS = CHUNKS * GROUPS
BANKS = 8

UNIT_TICKS = 4
CHUNK_TICKS = UNIT_TICKS * GROUPS
TICKS = UNIT_TICKS * UNITS
SCALAR_EVERY = 3
PREPARE_TICKS = UNIT_TICKS * (GROUPS + 1)
LAG = 3
QUANT_LAG = 5
SHADE_STEP = 2
RAD_STEP = 5
WARM_PASSES = 18


def tile_blinn_phong_radiance_features_k5_kernel(
    tc, nrm_words, nrm_scales, half_words, half_scales, radiance, specular, diffuse, out_0, out_1, out_2
):
    nc = tc.nc
    with ExitStack() as ctx:
        keep = ctx.enter_context(tc.tile_pool(name="keep", bufs=1))
        work = ctx.enter_context(tc.tile_pool(name="work", bufs=3))
        psum = ctx.enter_context(tc.psum_pool(name="psum", bufs=1))
        ctx.enter_context(tc.manual_schedule())

        taken = []

        def next_bank():
            bank = psum.tile([P, 512], F32, name="bank%d" % len(taken), tag="bank%d" % (len(taken) % BANKS))
            taken.append(bank)
            return bank

        def kept(shape, dtype, name):
            return keep.tile(shape, dtype, name=name, align_bytes=64)

        hw_raw = [kept([P, PASSES, 2 * K_PASS], U8, "hw_raw%d" % g) for g in range(GROUPS)]
        hs_raw = kept([P, PASSES, LIGHTS], U8, "hs_raw")
        aw = [kept([P, PASSES, 2 * CHUNK], U8, "aw%d" % c) for c in range(CHUNKS)]
        as_first = kept([P, PASSES, CHUNK], U8, "as_first")
        as_rest = kept([P, PASSES, POINTS - CHUNK], U8, "as_rest")
        rad_raw = [kept([P, SLOTS, RAD], BF16, "rad_raw%d" % g) for g in range(GROUPS)]
        dif = [kept([P, TILES, RAD], BF16, "dif%d" % c) for c in range(CHUNKS)]
        spec_raw = kept([POINTS // P, P], BF16, "spec_raw")
        spec_rows = kept([P, P], F32, "spec_rows")
        spec = kept([P, POINTS // P], F32, "spec")
        ident = kept([P, P], F32, "ident")

        def load_words(dst, words, block):
            src = words.bitcast(I32)[:, :, 256 * block : 256 * (block + 1)]
            nc.sync.dma_start(out=dst[:].bitcast(I32), in_=src.rearrange("k p w -> p k w"))

        def load_scales(dst, scales, col0, cols):
            for r in range(4):
                src = scales.bitcast(I32).rearrange("k (q r) w -> r q k w", r=4)[r]
                nc.sync.dma_start(out=dst[:].bitcast(I32)[r:P:32], in_=src[:, :, col0 // 4 : (col0 + cols) // 4])

        def load_radiance(g):
            src = radiance[K_PASS * g : K_PASS * (g + 1), :].rearrange("(j t b) f -> b j t f", t=SLOTS, b=4)
            for b in range(4):
                nc.sync.dma_start(out=rad_raw[g][b:P:4], in_=src[b])

        def load_diffuse(c):
            src = diffuse[CHUNK * c : CHUNK * (c + 1), :].rearrange("(j p) f -> p j f", p=P)
            nc.sync.dma_start(out=dif[c][:], in_=src)

        zeros = kept([P, K_PASS], BF16, "zeros")
        zero_codes = kept([P, P], U32, "zero_codes")
        zero_scales = kept([P, P], U8, "zero_scales")
        nc.vector.memset(hs_raw[:].bitcast(I32), 0)
        nc.vector.memset(as_first[:].bitcast(I32), 0)
        nc.vector.memset(zeros[:], 0.0)
        nc.vector.memset(as_rest[:].bitcast(I32), 0)

        nc.vector.quantize_mx(out=zero_codes[:].bitcast(FP8X4), scales=zero_scales[:], in_=zeros[:])
        warm_bank = next_bank()
        for warm_pass in range(WARM_PASSES):
            nc.tensor.matmul_mx(out=warm_bank[:, 0:P], lhsT=zero_codes[:].bitcast(FP8X4), lhsT_scale=zero_scales[:],
                                rhs=zero_codes[:].bitcast(FP8X4), rhs_scale=zero_scales[:], start=True, stop=True)

        load_words(hw_raw[0], half_words, 0)
        load_words(aw[0], nrm_words, 0)
        load_scales(hs_raw, half_scales, 0, LIGHTS)
        load_scales(as_first, nrm_scales, 0, CHUNK)
        load_words(hw_raw[1], half_words, 1)
        load_radiance(0)
        load_words(hw_raw[2], half_words, 2)
        nc.sync.dma_start(out=spec_raw[:], in_=specular.rearrange("(n p) -> n p", p=P))
        load_radiance(1)
        load_words(aw[1], nrm_words, 1)
        load_scales(as_rest, nrm_scales, CHUNK, POINTS - CHUNK)
        load_radiance(2)
        load_diffuse(0)
        for c in range(2, CHUNKS):
            load_words(aw[c], nrm_words, c)
        for c in range(1, CHUNKS):
            load_diffuse(c)

        make_identity(nc, ident[:])
        nc.gpsimd.memset(spec_rows[:], 0.0)
        nc.gpsimd.tensor_copy(out=spec_rows[0 : POINTS // P, :], in_=spec_raw[:])

        hw = [kept([P, PASSES, SLOTS, 2 * P], U8, "hw%d" % g) for g in range(GROUPS)]
        hs = kept([P, GROUPS, PASSES, SLOTS, P], U8, "hs")
        rad_codes = [kept([P, RAD], U32, "rad_codes%d" % g) for g in range(GROUPS)]
        rad_scales = [kept([P, RAD], U8, "rad_scales%d" % g) for g in range(GROUPS)]
        rad_il = [kept([P, RAD, SLOTS], BF16, "rad_il%d" % g) for g in range(GROUPS)]
        s_codes = [kept([P, CHUNK], U32, "s_codes%d" % u) for u in range(UNITS)]
        s_scales = [kept([P, CHUNK], U8, "s_scales%d" % u) for u in range(UNITS)]
        y_codes = [kept([P, CHUNK], U32, "y_codes%d" % c) for c in range(CHUNKS)]
        y_scales = kept([P, POINTS], U8, "y_scales")
        d_bank, c_bank, turned, relu_d, lobe, y, y_pairs, y_t = {}, {}, {}, {}, {}, {}, {}, {}
        words_out = out_1[0].rearrange("p m t -> p (m t)").bitcast(I32)

        def sort_lights(g):
            nc.vector.tensor_copy(
                out=hw[g][:].bitcast(I32).rearrange("p k t (j w) -> p k t j w", w=2),
                in_=hw_raw[g][:].bitcast(I32).rearrange("p k (j t w) -> p k t j w", t=SLOTS, w=2),
            )

        def sort_light_scales():
            nc.vector.tensor_copy(
                out=hs[:].bitcast(I32),
                in_=hs_raw[:].bitcast(I32).rearrange("p k (g j t) -> p g k t j", g=GROUPS, t=SLOTS),
            )

        def interleave_radiance(g):
            nc.vector.tensor_copy(out=rad_il[g][:].rearrange("p (c i) t -> p c t i", i=4),
                                  in_=rad_raw[g][:].rearrange("p t (c i) -> p c t i", i=4))

        def quantize_radiance(g):
            nc.vector.quantize_mx(out=rad_codes[g][:].bitcast(FP8X4), scales=rad_scales[g][:],
                                  in_=rad_il[g][:].rearrange("p f t -> p (f t)"))

        def spread_specular():
            bank = next_bank()
            nc.tensor.transpose(bank[:, 0:P], spec_rows[:], ident[:])
            nc.scalar.copy(out=spec[:], in_=bank[:, 0 : POINTS // P])

        def dots(tick):
            u, step = divmod(tick, UNIT_TICKS)
            c, g = divmod(u, GROUPS)
            h, pair = divmod(step, 2)
            d_bank[tick] = next_bank()
            for e in range(2):
                for k in range(PASSES):
                    a_scale = as_first[:, k, :] if c == 0 else as_rest[:, k, CHUNK * (c - 1) : CHUNK * c]
                    nc.tensor.matmul_mx(
                        out=d_bank[tick][:, HALF * e : HALF * (e + 1)],
                        lhsT=hw[g][:, k, 2 * pair + e, :].bitcast(FP4X4), lhsT_scale=hs[:, g, k, 2 * pair + e, :],
                        rhs=aw[c][:, k, 2 * HALF * h : 2 * HALF * (h + 1)].bitcast(FP4X4),
                        rhs_scale=a_scale[:, HALF * h : HALF * (h + 1)],
                        start=(k == 0), stop=(k == PASSES - 1))

        def relu(tick):
            u, step = divmod(tick, UNIT_TICKS)
            h, pair = divmod(step, 2)
            if pair == 0:
                relu_d[u, h] = work.tile([P, 2, HALF, 2], F32, name="rel%d_%d" % (u, h), tag="relu", bufs=8)
            dst = relu_d[u, h][:, pair, :, :]
            src = d_bank[tick][:].rearrange("p (e i) -> p i e", e=2)
            if tick % (2 if tick < PREPARE_TICKS else SCALAR_EVERY) == 0:
                nc.scalar.activation(out=dst, in_=src, func=ACT.Relu)
            else:
                nc.vector.tensor_scalar(out=dst, in0=src, scalar1=0.0, scalar2=None, op0=ALU.max)

        def square(u, c0, c1):
            if c0 == 0:
                lobe[u] = work.tile([P, CHUNK, SLOTS], BF16, name="lobe%d" % u, tag="lobe", align_bytes=64)
            h, first = divmod(c0, HALF)
            nc.scalar.activation(out=lobe[u][:, c0:c1, :].rearrange("p i (u e) -> p i u e", u=2),
                                 in_=relu_d[u, h][:, :, first : first + c1 - c0, :].rearrange("p u i e -> p i u e"),
                                 func=ACT.Square)

        def quantize_lobe(u, c0, c1):
            nc.vector.quantize_mx(out=s_codes[u][:, c0:c1].bitcast(FP8X4), scales=s_scales[u][:, c0:c1],
                                  in_=lobe[u][:, c0:c1, :].rearrange("p i t -> p (i t)"))

        def shade(n, g0, g1):
            c, j = divmod(n, TILES)
            if g0 == 0:
                c_bank[n] = next_bank()
            cols = slice(P * j, P * (j + 1))
            for g in range(g0, g1):
                u = GROUPS * c + g
                nc.tensor.matmul_mx(out=c_bank[n][:], lhsT=s_codes[u][:, cols].bitcast(FP8X4), lhsT_scale=s_scales[u][:, cols],
                                    rhs=rad_codes[g][:].bitcast(FP8X4), rhs_scale=rad_scales[g][:],
                                    start=(g == 0), stop=(g == GROUPS - 1))

        def finish(n):
            c, j = divmod(n, TILES)
            y[n] = work.tile([P, RAD], F32, name="y%d" % n, tag="y", bufs=6)
            nc.vector.scalar_tensor_tensor(out=y[n][:], in0=c_bank[n][:], scalar=spec[:, n : n + 1], in1=dif[c][:, j, :],
                                           op0=ALU.mult, op1=ALU.add)
            nc.sync.dma_start(out=out_0[P * n : P * (n + 1), :], in_=y[n][:])

        def round_pairs(n):
            y_pairs[n] = work.tile([P, 2, P, 2], BF16, name="y_pairs%d" % n, tag="y_pairs", bufs=8)
            src = y[n][:].rearrange("p (m u e) -> p u m e", u=2, e=2)
            if n == TILES * CHUNKS - 1:
                nc.vector.tensor_copy(out=y_pairs[n][:], in_=src)
            elif n == TILES * CHUNKS - 2:
                nc.scalar.copy(out=y_pairs[n][:], in_=src)
            else:
                nc.gpsimd.tensor_scalar(out=y_pairs[n][:], in0=src, scalar1=1.0, scalar2=0.0, op0=ALU.mult, op1=ALU.add)

        def turn(n0):
            turned[n0] = next_bank()
            for s in range(2):
                words = y_pairs[n0 + s][:].rearrange("p u m e -> p u (m e)").bitcast(F32)
                for u in range(2):
                    col = P * (2 * s + u)
                    nc.tensor.transpose(turned[n0][:, col : col + P], words[:, u, :], ident[:])

        def gather(n0):
            c, j = divmod(n0, TILES)
            if j == 0:
                y_t[c] = work.tile([P, CHUNK, SLOTS], BF16, name="y_t%d" % c, tag="y_t", align_bytes=64)
            dst = y_t[c][:, P * j : P * (j + 2), :].bitcast(F32).rearrange("p (s i) u -> p s i u", s=2)
            nc.scalar.copy(out=dst, in_=turned[n0][:].rearrange("p (s u i) -> p s i u", s=2, u=2))

        def quantize_result(c, c0, c1):
            cols = slice(CHUNK * c + c0, CHUNK * c + c1)
            nc.vector.quantize_mx(out=y_codes[c][:, c0:c1].bitcast(FP8X4), scales=y_scales[:, cols],
                                  in_=y_t[c][:, c0:c1, :].rearrange("p i t -> p (i t)"))
            nc.sync.dma_start(out=words_out[:, cols], in_=y_codes[c][:, c0:c1].bitcast(I32))

        steps = {}

        def at(tick, step, *args):
            if tick < TICKS:
                steps.setdefault(tick, []).append((step, args))

        def quant_tick(u):
            return UNIT_TICKS * (u + 1) + QUANT_LAG

        def shade_tick(n):
            c, j = divmod(n, TILES)
            put_off = CHUNK_TICKS - TILES * SHADE_STEP if c == 0 else 0
            return quant_tick(GROUPS * c + GROUPS - 1) + SHADE_STEP * (j + 1) + put_off

        def turn_tick(c):
            return shade_tick(TILES * c + TILES - 1) + 3 * LAG

        last = UNITS - 1
        tail = TILES * (CHUNKS - 1)
        for tick in range(TICKS):
            at(tick, dots, tick)
        at(CHUNK_TICKS, spread_specular)
        for c in range(CHUNKS - 1):
            for n in range(TILES * c, TILES * (c + 1)):
                at(shade_tick(n), shade, n, 0, GROUPS)
            at(turn_tick(c), turn, TILES * c)
            at(turn_tick(c), turn, TILES * c + 2)
        for u in range(last):
            at(quant_tick(u), quantize_lobe, u, 0, CHUNK)
        for n in range(tail):
            at(shade_tick(n) + LAG, finish, n)
        for tick in range(TICKS):
            at(tick + 1, relu, tick)
        for u in range(last):
            at(UNIT_TICKS * u + 4, square, u, 0, HALF)
            at(UNIT_TICKS * u + 6, square, u, HALF, CHUNK)
        at(0, sort_lights, 1)
        at(UNIT_TICKS + 1, sort_lights, 2)
        for g in range(GROUPS):
            at(2 + RAD_STEP * g, interleave_radiance, g)
            at(2 + RAD_STEP * g + LAG, quantize_radiance, g)
        for c in range(CHUNKS - 1):
            for n in range(TILES * c, TILES * (c + 1)):
                at(shade_tick(n) + 2 * LAG, round_pairs, n)
            at(turn_tick(c) + 1, gather, TILES * c)
            at(turn_tick(c) + 2, gather, TILES * c + 2)
            at(turn_tick(c) + 1 + LAG, quantize_result, c, 0, CHUNK)
        at(TICKS - 1, square, last, 0, P)
        at(TICKS - 1, square, last, P, HALF)

        sort_lights(0)
        sort_light_scales()
        for tick in range(TICKS):
            for step, args in steps[tick]:
                step(*args)

        relu(TICKS - 1)
        shade(tail - 1, 0, GROUPS)
        square(last, HALF, HALF + P)
        square(last, HALF + P, CHUNK)
        quantize_lobe(last - 1, 0, CHUNK)
        finish(tail - 3)
        round_pairs(tail - 4)
        gather(tail - TILES - 2)
        shade(tail, 0, GROUPS - 1)
        shade(tail + 1, 0, GROUPS - 1)
        quantize_lobe(last, 0, HALF)
        finish(tail - 2)
        round_pairs(tail - 3)
        shade(tail, GROUPS - 1, GROUPS)
        shade(tail + 1, GROUPS - 1, GROUPS)
        quantize_lobe(last, HALF, CHUNK)
        finish(tail - 1)
        round_pairs(tail - 2)
        shade(tail + 2, 0, GROUPS)
        shade(tail + 3, 0, GROUPS)
        round_pairs(tail - 1)
        for n0 in (tail - 4, tail - 2):
            turn(n0)
        for n0 in (tail - 4, tail - 2):
            gather(n0)
        for n in range(tail, tail + TILES - 1):
            finish(n)
            round_pairs(n)
        turn(tail)
        gather(tail)
        finish(tail + 3)
        round_pairs(tail + 3)
        turn(tail + 2)
        quantize_result(CHUNKS - 3, 0, CHUNK)
        gather(tail + 2)
        quantize_result(CHUNKS - 2, 0, CHUNK)
        quantize_result(CHUNKS - 1, 0, HALF)
        quantize_result(CHUNKS - 1, HALF, CHUNK)
        for q in range(4):
            queue = nc.scalar if q % 2 else nc.sync
            queue.dma_start(out=out_2[0].bitcast(I32)[4 * q : 4 * q + 4, :], in_=y_scales[:].bitcast(I32)[32 * q : 32 * q + 4, :])
